import numpy as np
import ml_dtypes


def mxq(x, axis, fmt="e4m3"):
    dtype, down = {"e4m3": (ml_dtypes.float8_e4m3fn, 7), "e5m2": (ml_dtypes.float8_e5m2, 14)}[fmt]
    v = np.moveaxis(np.asarray(x, np.float32).astype(ml_dtypes.bfloat16).astype(np.float64), axis, -1)
    blocks = v.reshape(v.shape[:-1] + (-1, 32))
    amax = np.abs(blocks).max(-1, keepdims=True)
    byte = np.maximum(np.where(amax > 0, np.frexp(amax)[1] - 1 + 127, 0) - down, 1)
    scale = np.exp2(byte - 127.0)
    codes = (blocks / scale).astype(np.float32).astype(dtype).astype(np.float64)
    return np.moveaxis((codes * scale).reshape(v.shape), -1, axis)


WIDE = False


def mx_kscale(k):
    if not WIDE:
        return np.ones(k)
    levels = np.array([10, -10, 5, -5, 0])
    if k % 512:
        return np.exp2(np.random.permutation(np.resize(levels, k // 32))).repeat(32)
    a = np.empty((k // 512, 16))
    for p in range(k // 512):
        a[p, :8] = np.random.permutation(np.resize(levels, 8))
        for g in range(8):
            far = levels[np.abs(levels - a[p, g]) >= 10]
            a[p, g + 8] = far[np.random.randint(len(far))]
    return np.exp2(a.ravel()).repeat(32)


def f64(x):
    return np.asarray(x).astype(np.float64)


def striped(idx):
    return np.tile(idx.reshape(-1, 16).T, (8, 1)).astype(np.uint16)


def unstriped(offs):
    return offs[:16].T.reshape(-1).astype(np.int64)


def striped8(idx):
    return np.concatenate([x.reshape(-1, 16).T for x in idx]).astype(np.uint16)


def runs(offs, k):
    lists = np.stack([offs[16 * r : 16 * r + 16].T.reshape(-1) for r in range(8)]).astype(np.int64)
    return lists[np.arange(k) % 512 // 64]


def pack_weight(w):
    k, n = w.shape
    w = f64(np.asarray(w, np.float32).astype(ml_dtypes.bfloat16)).reshape(k // 32, 32, n)
    amax = np.abs(w).max(1)
    byte = np.clip(np.where(amax > 0, np.frexp(amax)[1] - 1 + 127 - 7, 1), 1, 254)
    scaled = (w * np.exp2(127.0 - byte)[:, None, :]).reshape(k, n).astype(np.float32)
    words = np.ascontiguousarray(scaled.reshape(k // 512, 128, 4, n).transpose(0, 1, 3, 2)).astype(ml_dtypes.float8_e4m3fn).view(np.uint8)
    return words, np.ascontiguousarray(byte.astype(np.uint8).reshape(k // 512, 16, n))


def unpack_weight(words, scales):
    g, p, n, _ = words.shape
    vals = np.ascontiguousarray(words).view(ml_dtypes.float8_e4m3fn).astype(np.float64) * np.repeat(np.exp2(scales.astype(np.float64) - 127.0), 8, axis=1)[..., None]
    return vals.transpose(0, 1, 3, 2).reshape(g * 512, n)


K, T, S, H, W, G = 512, 2048, 512, 512, 256, 2048


def setup_inputs():
    n = np.random.standard_normal
    s = mx_kscale(K)[:, None]
    packed_xT = pack_weight(n((K, T)) * s)
    packed_dT = pack_weight(n((K, G)) / s)
    perm = np.random.permutation(S)
    return {
        "x_words": packed_xT[0],
        "x_scales": packed_xT[1],
        "w1": (n((K, H)) / np.sqrt(K) / s).astype(np.float32),
        "gs": (np.random.uniform(0.5, 1.5, (K, 1)) * s).astype(np.float32),
        "d_words": packed_dT[0],
        "d_scales": packed_dT[1],
        "offs": striped(np.random.permutation(T)[:S]),
        "n1": striped(perm[:W]),
        "n2": striped(perm[W:]),
        "ka": striped8(np.random.randint(0, G, (8, H))),
        "kb": striped8(np.random.randint(0, G, (8, H))),
        "n3": striped8(np.stack([np.random.permutation(S) for _ in range(8)])),
        "n4": striped8(np.stack([np.random.permutation(S) for _ in range(8)])),
    }


def reference(x_words, x_scales, w1, gs, d_words, d_scales, offs, n1, n2, ka, kb, n3, n4):
    d_ka = unpack_weight(d_words, d_scales)[np.arange(K)[:, None], runs(ka, K)]
    xq = unpack_weight(x_words, x_scales)[:, unstriped(offs)]
    y = mxq(f64(w1), 0, "e4m3").T @ xq
    pa = y[:, unstriped(n1)]
    pb = y[:, unstriped(n2)]
    rb = pa - pb
    ra = 0.75 * (pa + pb)
    ds = np.zeros((H, S))
    ds[:, unstriped(n1)] = ra
    dt = ds.copy()
    dt[:, unstriped(n2)] = rb
    z = f64(gs) * dt
    zq = mxq(z, 0, "e4m3")
    d_kb = unpack_weight(d_words, d_scales)[np.arange(K)[:, None], runs(kb, K)]
    h = 0.0625 * (d_ka.T @ zq + d_kb.T @ zq)
    ds2 = np.zeros((H, S))
    ds2[np.arange(H)[:, None], runs(n3, H)] = h
    return np.maximum(h, ds2[np.arange(H)[:, None], runs(n4, H)])

@@ -1,0 +1,211 @@
+from contextlib import ExitStack
+
+import concourse.mybir as mybir
+
+K, T, S, H, W, G = 512, 2048, 512, 512, 256, 2048
+FLOPS = 3 * 2 * K * H * S
+
+F32 = mybir.dt.float32
+BF16 = mybir.dt.bfloat16
+I32 = mybir.dt.int32
+U32 = mybir.dt.uint32
+U16 = mybir.dt.uint16
+U8 = mybir.dt.uint8
+FP8X4 = mybir.dt.float8_e4m3fn_x4
+COPY = mybir.ActivationFunctionType.Copy
+ADD = mybir.AluOpType.add
+MAX = mybir.AluOpType.max
+
+P = 128
+PACK = 4
+HALF = S // 2
+
+
+def tile_picked_daqhaarrelay_none_p_kernel(
+    tc, x_words, x_scales, w1, gs, d_words, d_scales, offs, n1, n2, ka, kb, n3, n4, out
+):
+    nc = tc.nc
+    with ExitStack() as ctx:
+        lists = ctx.enter_context(tc.tile_pool(name="lists", bufs=1))
+        keep = ctx.enter_context(tc.tile_pool(name="keep", bufs=1))
+        relay = ctx.enter_context(tc.tile_pool(name="relay", bufs=1))
+        psum = ctx.enter_context(tc.psum_pool(name="psum", bufs=8))
+
+        def alloc(name, shape, dtype, tag=None):
+            return keep.tile(shape, dtype, name=name, tag=tag or name, align_bytes=64)
+
+        def load_list(name, src):
+            t = lists.tile(list(src.shape), U16, name=name)
+            nc.sync.dma_start(t[:], src)
+            return t
+
+        def half_cols(u):
+            return slice(u * HALF, (u + 1) * HALF)
+
+        def half_list(lst, u):
+            return lst[:, u * HALF // 16 : (u + 1) * HALF // 16]
+
+        d_bytes = alloc("d_bytes", [P, G], U8)
+        x_bytes = alloc("x_bytes", [P, T], U8)
+        d_plane = alloc("d_plane", [P, 2 * H], U8)
+        nc.vector.memset(d_bytes[:].bitcast(I32), 0)
+        nc.vector.memset(x_bytes[:].bitcast(I32), 0)
+        nc.gpsimd.memset(d_plane[:].bitcast(I32), 0)
+
+        ka_l = load_list("ka_l", ka)
+        kb_l = load_list("kb_l", kb)
+        w_rows = w1.rearrange("(p j) c -> p j c", j=PACK)
+        w_raw = [alloc(f"w_raw{u}", [P, PACK, HALF], F32) for u in range(2)]
+        nc.sync.dma_start(w_raw[0][:], w_rows[:, :, half_cols(0)])
+        nc.sync.dma_start(d_bytes[0:P:8, :].bitcast(I32), d_scales[0].bitcast(I32))
+        for q in range(4):
+            nc.sync.dma_start(x_bytes[32 * q : 32 * q + 4, :].bitcast(I32), x_scales[0, 4 * q : 4 * q + 4, :].bitcast(I32))
+        nc.sync.dma_start(w_raw[1][:], w_rows[:, :, half_cols(1)])
+        offs_l = load_list("offs_l", offs)
+        x_table = alloc("x_table", [P, T], I32)
+        nc.sync.dma_start(x_table[:], x_words[0].rearrange("p n t -> p (n t)").bitcast(I32))
+        n2_l = load_list("n2_l", n2)
+        n1_l = load_list("n1_l", n1)
+        d_table = alloc("d_table", [P, G], I32)
+        nc.sync.dma_start(d_table[:], d_words[0].rearrange("p n t -> p (n t)").bitcast(I32))
+        n3_l = load_list("n3_l", n3)
+        n4_l = load_list("n4_l", n4)
+        gain = alloc("gain", [P, PACK], F32)
+        nc.sync.dma_start(gain[:], gs.rearrange("(p t) o -> p (t o)", t=PACK))
+
+        d_picked_bytes = alloc("d_picked_bytes", [P, 2 * H], U8)
+        for a, lst in enumerate((ka_l, kb_l)):
+            nc.vector.tensor_copy(d_picked_bytes[:, a * H : (a + 1) * H], d_bytes[:].indirect(lst[:]))
+        x_plane = alloc("x_plane", [P, S], U8)
+        nc.vector.tensor_copy(x_plane[:], x_bytes[:].indirect(offs_l[:]))
+
+        w_bf = alloc("w_bf", [P, PACK, P, PACK], BF16)
+        for u in range(2):
+            nc.scalar.activation(
+                w_bf[:, :, u * 64 : (u + 1) * 64, :].rearrange("p t m j -> p m t j"),
+                w_raw[u][:].rearrange("p j (m t) -> p m t j", t=PACK),
+                COPY,
+            )
+        w_codes = alloc("w_codes", [P, H], U32)
+        w_plane = alloc("w_plane", [P, H], U8)
+        nc.vector.quantize_mx(w_codes[:].bitcast(FP8X4), w_plane[:], w_bf[:].rearrange("p t m j -> p (t m j)"))
+
+        x_codes = alloc("x_codes", [P, S], U32)
+        for u in range(2):
+            nc.vector.tensor_copy(x_codes[:, half_cols(u)], x_table[:].bitcast(U32).indirect(half_list(offs_l, u)))
+
+        def product_y(t, cols, y):
+            width = cols.stop - cols.start
+            bank = psum.tile([P, S], F32, name="bank")
+            rows = slice(t * P, (t + 1) * P)
+            nc.tensor.matmul_mx(
+                bank[:, :width], w_codes[:, rows].bitcast(FP8X4), w_plane[:, rows],
+                x_codes[:, cols].bitcast(FP8X4), x_plane[:, cols], start=True, stop=True,
+            )
+            nc.scalar.activation(y[:, cols], bank[:, :width], COPY)
+
+        d_dealt_bytes = alloc("d_dealt_bytes", [P, 2 * H], U8)
+        nc.vector.tensor_copy(
+            d_dealt_bytes[:].rearrange("p (a t m) -> p a m t", a=2, t=PACK),
+            d_picked_bytes[:].rearrange("p (a m t) -> p a m t", a=2, t=PACK),
+        )
+        for q in range(4):
+            nc.sync.dma_start(d_plane[32 * q : 32 * q + 4, :].bitcast(I32), d_dealt_bytes[32 * q : 32 * q + 32 : 8, :].bitcast(I32))
+
+        def pick_codes(name, lst, tag):
+            picked = alloc(name, [P, H], U32, tag)
+            nc.vector.tensor_copy(picked[:], d_table[:].bitcast(U32).indirect(lst[:]))
+            return picked
+
+        def deal_codes(dealt, picked, t0, t1):
+            nc.vector.tensor_copy(
+                dealt[:].bitcast(I32).rearrange("p (t m) -> p m t", t=PACK)[:, :, t0:t1],
+                picked[:].bitcast(I32).rearrange("p (m t) -> p m t", t=PACK)[:, :, t0:t1],
+            )
+
+        a_picked = pick_codes("a_picked", ka_l, None)
+        a_codes = alloc("a_codes", [P, H], U32)
+        deal_codes(a_codes, a_picked, 0, PACK)
+
+        def place_sums(dt, scaled):
+            nc.vector.tensor_tensor(dt[:].indirect(n1_l[:]), scaled[:, 0, :], scaled[:, 1, :], ADD)
+
+        placed = []
+        for t in range(PACK):
+            y = relay.tile([P, S], F32, name=f"y{t}", offset=(2048, 1024, 3072, 1024)[t], align_bytes=64)
+            for cols in (half_cols(0), half_cols(1)) if t == 0 else (slice(0, S),):
+                product_y(t, cols, y)
+            pa = alloc(f"pa{t}", [P, W], F32)
+            pb_neg = alloc(f"pb_neg{t}", [P, W], F32)
+            nc.scalar.activation(pa[:], y[:].indirect(n1_l[:]), COPY)
+            nc.scalar.activation(pb_neg[:], y[:].indirect(n2_l[:]), COPY, scale=-1.0)
+            scaled = alloc(f"scaled{t}", [P, 2, W], F32)
+            nc.scalar.activation(scaled[:, 0, :], pa[:], COPY, scale=0.75)
+            nc.scalar.activation(scaled[:, 1, :], pb_neg[:], COPY, scale=-0.75)
+            dt = alloc(f"dt{t}", [P, S], F32, "a_picked" if t == 0 else f"pb_neg{t - 1}")
+            nc.vector.tensor_tensor(dt[:].indirect(n2_l[:]), pa[:], pb_neg[:], ADD)
+            if placed:
+                place_sums(*placed[-1])
+            placed.append((dt, scaled))
+        place_sums(*placed[-1])
+
+        pairs = [relay.tile([P, 2, 2 * HALF], BF16, name=f"pairs{u}", offset=2048 * u, align_bytes=64) for u in range(2)]
+        for t, (dt, scaled) in enumerate(placed):
+            for u in range(2):
+                nc.scalar.activation(pairs[u][:, t // 2, t % 2 :: 2], dt[:, half_cols(u)], COPY, scale=gain[:, t : t + 1])
+
+        b_picked = pick_codes("b_picked", kb_l, f"scaled{PACK - 1}")
+        b_codes = alloc("b_codes", [P, H], U32)
+        deal_codes(b_codes, b_picked, 0, 1)
+
+        z_codes = alloc("z_codes", [P, S], U32)
+        z_plane = alloc("z_plane", [P, S], U8)
+        for u in range(2):
+            z_bf = alloc(f"z_bf{u}", [P, HALF * PACK], BF16)
+            nc.vector.tensor_copy(
+                z_bf[:].bitcast(I32).rearrange("p (c v) -> p c v", v=2),
+                pairs[u][:].bitcast(I32).rearrange("p v c -> p c v"),
+            )
+            nc.vector.quantize_mx(z_codes[:, half_cols(u)].bitcast(FP8X4), z_plane[:, half_cols(u)], z_bf[:])
+
+        deal_codes(b_codes, b_picked, 1, PACK)
+
+        out_rows = out.rearrange("(p t) c -> t p c", t=PACK)
+
+        def product_h(t, cols, h):
+            width = cols.stop - cols.start
+            bank = psum.tile([P, S], F32, name="bank")
+            rows = slice(t * P, (t + 1) * P)
+            for a, codes in enumerate((a_codes, b_codes)):
+                nc.tensor.matmul_mx(
+                    bank[:, :width], codes[:, rows].bitcast(FP8X4), d_plane[:, a * H + t * P : a * H + (t + 1) * P],
+                    z_codes[:, cols].bitcast(FP8X4), z_plane[:, cols], start=(a == 0), stop=(a == 1),
+                )
+            nc.scalar.activation(h[:, cols], bank[:, :width], COPY, scale=0.0625)
+
+        def finish(t, h, ds2, pieces):
+            for cols, lst in pieces:
+                width = cols.stop - cols.start
+                fetched = alloc(f"fetched{t}_{cols.start}", [P, width], F32)
+                nc.scalar.activation(fetched[:], ds2[:].indirect(lst), COPY)
+                res = alloc(f"res{t}_{cols.start}", [P, width], F32)
+                nc.vector.tensor_tensor(res[:], h[:, cols], fetched[:], MAX)
+                nc.sync.dma_start(out_rows[t][:, cols], res[:])
+
+        whole = lambda lst: [(slice(0, S), lst[:])]
+        halves = lambda lst: [(half_cols(u), half_list(lst, u)) for u in range(2)]
+        hs = []
+        for t in range(PACK):
+            h = alloc(f"h{t}", [P, S], F32)
+            for cols, lst in halves(n3_l) if t == 0 else whole(n3_l):
+                product_h(t, cols, h)
+            hs.append(h)
+        pending = None
+        for t, h in enumerate(hs):
+            ds2 = alloc(f"ds2_{t}", [P, 2 * S], F32)
+            for cols, lst in halves(n3_l) if t == 0 else whole(n3_l):
+                nc.vector.tensor_copy(ds2[:].indirect(lst), h[:, cols])
+            if pending is not None:
+                finish(*pending, whole(n4_l))
+            pending = (t, h, ds2)
+        finish(*pending, halves(n4_l))

@@ -48,16 +48,15 @@ def tile_picked_daqhaarrelay_none_p_kernel(
         d_bytes = alloc("d_bytes", [P, G], U8)
         x_bytes = alloc("x_bytes", [P, T], U8)
         d_plane = alloc("d_plane", [P, 2 * H], U8)
-        nc.vector.memset(d_bytes[:].bitcast(I32), 0)
         nc.vector.memset(x_bytes[:].bitcast(I32), 0)
         nc.gpsimd.memset(d_plane[:].bitcast(I32), 0)
 
         ka_l = load_list("ka_l", ka)
+        nc.sync.dma_start(d_bytes[:].bitcast(I32), d_scales[0].bitcast(I32).unsqueeze(1).to_broadcast([16, 8, G // 4]))
         kb_l = load_list("kb_l", kb)
         w_rows = w1.rearrange("(p j) c -> p j c", j=PACK)
         w_raw = [alloc(f"w_raw{u}", [P, PACK, HALF], F32) for u in range(2)]
         nc.sync.dma_start(w_raw[0][:], w_rows[:, :, half_cols(0)])
-        nc.sync.dma_start(d_bytes[0:P:8, :].bitcast(I32), d_scales[0].bitcast(I32))
         for q in range(4):
             nc.sync.dma_start(x_bytes[32 * q : 32 * q + 4, :].bitcast(I32), x_scales[0, 4 * q : 4 * q + 4, :].bitcast(I32))
         nc.sync.dma_start(w_raw[1][:], w_rows[:, :, half_cols(1)])
@@ -104,59 +103,87 @@ def tile_picked_daqhaarrelay_none_p_kernel(
             )
             nc.scalar.activation(y[:, cols], bank[:, :width], COPY)
 
-        d_dealt_bytes = alloc("d_dealt_bytes", [P, 2 * H], U8)
-        nc.vector.tensor_copy(
-            d_dealt_bytes[:].rearrange("p (a t m) -> p a m t", a=2, t=PACK),
-            d_picked_bytes[:].rearrange("p (a m t) -> p a m t", a=2, t=PACK),
-        )
-        for q in range(4):
-            nc.sync.dma_start(d_plane[32 * q : 32 * q + 4, :].bitcast(I32), d_dealt_bytes[32 * q : 32 * q + 32 : 8, :].bitcast(I32))
-
-        def pick_codes(name, lst, tag):
-            picked = alloc(name, [P, H], U32, tag)
-            nc.vector.tensor_copy(picked[:], d_table[:].bitcast(U32).indirect(lst[:]))
-            return picked
-
-        def deal_codes(dealt, picked, t0, t1):
+        def deal_bytes(a, tag):
+            dealt = alloc(f"dealt_bytes{a}", [P, H], U8, tag)
             nc.vector.tensor_copy(
-                dealt[:].bitcast(I32).rearrange("p (t m) -> p m t", t=PACK)[:, :, t0:t1],
+                dealt[:].rearrange("p (t m) -> p m t", t=PACK),
+                d_picked_bytes[:, a * H : (a + 1) * H].rearrange("p (m t) -> p m t", t=PACK),
+            )
+            for q in range(4):
+                nc.sync.dma_start(
+                    d_plane[32 * q : 32 * q + 4, a * H : (a + 1) * H].bitcast(I32), dealt[32 * q : 32 * q + 32 : 8, :].bitcast(I32)
+                )
+
+        def deal_codes(dealt, picked, m0, t0, t1):
+            count = picked.shape[1] // PACK
+            nc.vector.tensor_copy(
+                dealt[:].bitcast(I32).rearrange("p (t m) -> p m t", t=PACK)[:, m0 : m0 + count, t0:t1],
                 picked[:].bitcast(I32).rearrange("p (m t) -> p m t", t=PACK)[:, :, t0:t1],
             )
 
-        a_picked = pick_codes("a_picked", ka_l, None)
+        deal_bytes(0, "x_table")
+        a_picked = [alloc(f"a_picked{u}", [P, HALF], U32) for u in range(2)]
         a_codes = alloc("a_codes", [P, H], U32)
-        deal_codes(a_codes, a_picked, 0, PACK)
+        for u in range(2):
+            nc.vector.tensor_copy(a_picked[u][:], d_table[:].bitcast(U32).indirect(half_list(ka_l, u)))
+        for u in range(2):
+            deal_codes(a_codes, a_picked[u], u * 64, 0, PACK)
 
-        def place_sums(dt, scaled):
-            nc.vector.tensor_tensor(dt[:].indirect(n1_l[:]), scaled[:, 0, :], scaled[:, 1, :], ADD)
+        y_at = (3584, 2048, 5120, 2048)
+        sum_at = (None, 6144, 2560, None)
+        dt_on = ("a_picked0", "pb_neg0", "pa0", "pb_neg1")
 
-        placed = []
-        for t in range(PACK):
-            y = relay.tile([P, S], F32, name=f"y{t}", offset=(2048, 1024, 3072, 1024)[t], align_bytes=64)
+        def fetch_pairs(t):
+            y = relay.tile([P, S], F32, name=f"y{t}", offset=y_at[t], align_bytes=64)
             for cols in (half_cols(0), half_cols(1)) if t == 0 else (slice(0, S),):
                 product_y(t, cols, y)
             pa = alloc(f"pa{t}", [P, W], F32)
             pb_neg = alloc(f"pb_neg{t}", [P, W], F32)
             nc.scalar.activation(pa[:], y[:].indirect(n1_l[:]), COPY)
             nc.scalar.activation(pb_neg[:], y[:].indirect(n2_l[:]), COPY, scale=-1.0)
-            scaled = alloc(f"scaled{t}", [P, 2, W], F32)
-            nc.scalar.activation(scaled[:, 0, :], pa[:], COPY, scale=0.75)
-            nc.scalar.activation(scaled[:, 1, :], pb_neg[:], COPY, scale=-0.75)
-            dt = alloc(f"dt{t}", [P, S], F32, "a_picked" if t == 0 else f"pb_neg{t - 1}")
+            return pa, pb_neg
+
+        def scale_pairs(t, pa, pb_neg):
+            if sum_at[t] is None:
+                pa_s = alloc(f"pa_s{t}", [P, W], F32)
+            else:
+                pa_s = relay.tile([P, W], F32, name=f"pa_s{t}", offset=sum_at[t], align_bytes=64)
+            pb_s = alloc(f"pb_s{t}", [P, W], F32)
+            nc.scalar.activation(pa_s[:], pa[:], COPY, scale=0.75)
+            nc.scalar.activation(pb_s[:], pb_neg[:], COPY, scale=-0.75)
+            return pa_s, pb_s
+
+        placed = []
+
+        def place_differences(t):
+            pa, pb_neg = fetch_pairs(t)
+            scaled = scale_pairs(t, pa, pb_neg) if t == 0 else None
+            dt = alloc(f"dt{t}", [P, S], F32, dt_on[t])
             nc.vector.tensor_tensor(dt[:].indirect(n2_l[:]), pa[:], pb_neg[:], ADD)
-            if placed:
-                place_sums(*placed[-1])
-            placed.append((dt, scaled))
-        place_sums(*placed[-1])
+            placed.append((dt, pa, pb_neg, scaled))
 
-        pairs = [relay.tile([P, 2, 2 * HALF], BF16, name=f"pairs{u}", offset=2048 * u, align_bytes=64) for u in range(2)]
-        for t, (dt, scaled) in enumerate(placed):
+        def place_sums(t):
+            dt, pa, pb_neg, scaled = placed[t]
+            pa_s, pb_s = scaled or scale_pairs(t, pa, pb_neg)
+            nc.vector.tensor_tensor(dt[:].indirect(n1_l[:]), pa_s[:], pb_s[:], ADD)
+
+        place_differences(0)
+        deal_bytes(1, "a_picked1")
+        place_sums(0)
+        place_differences(1)
+        for t in range(1, PACK):
+            if t + 1 < PACK:
+                place_differences(t + 1)
+            place_sums(t)
+
+        pairs = [relay.tile([P, 2, 2 * HALF], BF16, name=f"pairs{u}", offset=(64, 4032)[u], align_bytes=64) for u in range(2)]
+        for t in range(PACK):
             for u in range(2):
-                nc.scalar.activation(pairs[u][:, t // 2, t % 2 :: 2], dt[:, half_cols(u)], COPY, scale=gain[:, t : t + 1])
+                nc.scalar.activation(pairs[u][:, t // 2, t % 2 :: 2], placed[t][0][:, half_cols(u)], COPY, scale=gain[:, t : t + 1])
 
-        b_picked = pick_codes("b_picked", kb_l, f"scaled{PACK - 1}")
-        b_codes = alloc("b_codes", [P, H], U32)
-        deal_codes(b_codes, b_picked, 0, 1)
+        b_picked = alloc("b_picked", [P, H], U32, f"pb_s{PACK - 2}")
+        nc.vector.tensor_copy(b_picked[:], d_table[:].bitcast(U32).indirect(kb_l[:]))
+        b_codes = alloc("b_codes", [P, H], U32, dt_on[PACK - 1])
 
         z_codes = alloc("z_codes", [P, S], U32)
         z_plane = alloc("z_plane", [P, S], U8)
@@ -166,9 +193,8 @@ def tile_picked_daqhaarrelay_none_p_kernel(
                 z_bf[:].bitcast(I32).rearrange("p (c v) -> p c v", v=2),
                 pairs[u][:].bitcast(I32).rearrange("p v c -> p c v"),
             )
+            deal_codes(b_codes, b_picked, 0, *((0, 1), (1, PACK))[u])
             nc.vector.quantize_mx(z_codes[:, half_cols(u)].bitcast(FP8X4), z_plane[:, half_cols(u)], z_bf[:])
-
-        deal_codes(b_codes, b_picked, 1, PACK)
 
         out_rows = out.rearrange("(p t) c -> t p c", t=PACK)
 
@@ -194,18 +220,14 @@ def tile_picked_daqhaarrelay_none_p_kernel(
 
         whole = lambda lst: [(slice(0, S), lst[:])]
         halves = lambda lst: [(half_cols(u), half_list(lst, u)) for u in range(2)]
-        hs = []
-        for t in range(PACK):
-            h = alloc(f"h{t}", [P, S], F32)
-            for cols, lst in halves(n3_l) if t == 0 else whole(n3_l):
-                product_h(t, cols, h)
-            hs.append(h)
-        pending = None
-        for t, h in enumerate(hs):
-            ds2 = alloc(f"ds2_{t}", [P, 2 * S], F32)
-            for cols, lst in halves(n3_l) if t == 0 else whole(n3_l):
-                nc.vector.tensor_copy(ds2[:].indirect(lst), h[:, cols])
-            if pending is not None:
-                finish(*pending, whole(n4_l))
-            pending = (t, h, ds2)
-        finish(*pending, halves(n4_l))
+        hs = [alloc(f"h{t}", [P, S], F32) for t in range(PACK)]
+        ds2 = [alloc(f"ds2_{t}", [P, 2 * S], F32) for t in range(PACK)]
+        steps = [(0, *halves(n3_l)[0]), (1, *whole(n3_l)[0]), (0, *halves(n3_l)[1]), (2, *whole(n3_l)[0]), (3, *whole(n3_l)[0])]
+        for t, cols, lst in steps:
+            product_h(t, cols, hs[t])
+        after = {2: 1, 3: 0, 4: 2}
+        for n, (t, cols, lst) in enumerate(steps):
+            nc.vector.tensor_copy(ds2[t][:].indirect(lst), hs[t][:, cols])
+            if n in after:
+                finish(after[n], hs[after[n]], ds2[after[n]], whole(n4_l))
+        finish(3, hs[3], ds2[3], halves(n4_l))

@@ -13,12 +13,25 @@ U16 = mybir.dt.uint16
 U8 = mybir.dt.uint8
 FP8X4 = mybir.dt.float8_e4m3fn_x4
 COPY = mybir.ActivationFunctionType.Copy
+RELU = mybir.ActivationFunctionType.Relu
 ADD = mybir.AluOpType.add
+SUBTRACT = mybir.AluOpType.subtract
 MAX = mybir.AluOpType.max
 
 P = 128
 PACK = 4
+QUAD = 32
+BLOCK = 8
+STRIPE = 16
 HALF = S // 2
+HALVES = (slice(0, HALF), slice(HALF, S))
+WHOLE = slice(0, S)
+
+ROW = 4 * S
+EDGE = 64
+Y_AT = (7 * ROW // 4, ROW, 5 * ROW // 2, ROW)
+SCALED_AT = {1: 3 * ROW, 2: 5 * ROW // 4}
+PAIRS_AT = (EDGE, 2 * ROW - EDGE)
 
 
 def tile_picked_daqhaarrelay_none_p_kernel(
@@ -31,19 +44,16 @@ def tile_picked_daqhaarrelay_none_p_kernel(
         relay = ctx.enter_context(tc.tile_pool(name="relay", bufs=1))
         psum = ctx.enter_context(tc.psum_pool(name="psum", bufs=8))
 
-        def alloc(name, shape, dtype, tag=None):
-            return keep.tile(shape, dtype, name=name, tag=tag or name, align_bytes=64)
+        def alloc(name, shape, dtype, on=None):
+            return keep.tile(shape, dtype, name=name, tag=on or name, align_bytes=64)
 
         def load_list(name, src):
-            t = lists.tile(list(src.shape), U16, name=name)
-            nc.sync.dma_start(t[:], src)
-            return t
+            held = lists.tile(list(src.shape), U16, name=name)
+            nc.sync.dma_start(held[:], src)
+            return held
 
-        def half_cols(u):
-            return slice(u * HALF, (u + 1) * HALF)
-
-        def half_list(lst, u):
-            return lst[:, u * HALF // 16 : (u + 1) * HALF // 16]
+        def entries(held, cols):
+            return held[:, cols.start // STRIPE : cols.stop // STRIPE]
 
         d_bytes = alloc("d_bytes", [P, G], U8)
         x_bytes = alloc("x_bytes", [P, T], U8)
@@ -52,14 +62,18 @@ def tile_picked_daqhaarrelay_none_p_kernel(
         nc.gpsimd.memset(d_plane[:].bitcast(I32), 0)
 
         ka_l = load_list("ka_l", ka)
-        nc.sync.dma_start(d_bytes[:].bitcast(I32), d_scales[0].bitcast(I32).unsqueeze(1).to_broadcast([16, 8, G // 4]))
+        nc.sync.dma_start(
+            d_bytes[:].bitcast(I32), d_scales[0].bitcast(I32).unsqueeze(1).to_broadcast([P // BLOCK, BLOCK, G // 4])
+        )
         kb_l = load_list("kb_l", kb)
         w_rows = w1.rearrange("(p j) c -> p j c", j=PACK)
         w_raw = [alloc(f"w_raw{u}", [P, PACK, HALF], F32) for u in range(2)]
-        nc.sync.dma_start(w_raw[0][:], w_rows[:, :, half_cols(0)])
-        for q in range(4):
-            nc.sync.dma_start(x_bytes[32 * q : 32 * q + 4, :].bitcast(I32), x_scales[0, 4 * q : 4 * q + 4, :].bitcast(I32))
-        nc.sync.dma_start(w_raw[1][:], w_rows[:, :, half_cols(1)])
+        nc.sync.dma_start(w_raw[0][:], w_rows[:, :, HALVES[0]])
+        for q in range(P // QUAD):
+            nc.sync.dma_start(
+                x_bytes[QUAD * q : QUAD * q + PACK, :].bitcast(I32), x_scales[0, PACK * q : PACK * (q + 1), :].bitcast(I32)
+            )
+        nc.sync.dma_start(w_raw[1][:], w_rows[:, :, HALVES[1]])
         offs_l = load_list("offs_l", offs)
         x_table = alloc("x_table", [P, T], I32)
         nc.sync.dma_start(x_table[:], x_words[0].rearrange("p n t -> p (n t)").bitcast(I32))
@@ -73,15 +87,15 @@ def tile_picked_daqhaarrelay_none_p_kernel(
         nc.sync.dma_start(gain[:], gs.rearrange("(p t) o -> p (t o)", t=PACK))
 
         d_picked_bytes = alloc("d_picked_bytes", [P, 2 * H], U8)
-        for a, lst in enumerate((ka_l, kb_l)):
-            nc.vector.tensor_copy(d_picked_bytes[:, a * H : (a + 1) * H], d_bytes[:].indirect(lst[:]))
+        for a, held in enumerate((ka_l, kb_l)):
+            nc.vector.tensor_copy(d_picked_bytes[:, a * H : (a + 1) * H], d_bytes[:].indirect(held[:]))
         x_plane = alloc("x_plane", [P, S], U8)
         nc.vector.tensor_copy(x_plane[:], x_bytes[:].indirect(offs_l[:]))
 
         w_bf = alloc("w_bf", [P, PACK, P, PACK], BF16)
         for u in range(2):
             nc.scalar.activation(
-                w_bf[:, :, u * 64 : (u + 1) * 64, :].rearrange("p t m j -> p m t j"),
+                w_bf[:, :, u * P // 2 : (u + 1) * P // 2, :].rearrange("p t m j -> p m t j"),
                 w_raw[u][:].rearrange("p j (m t) -> p m t j", t=PACK),
                 COPY,
             )
@@ -90,28 +104,19 @@ def tile_picked_daqhaarrelay_none_p_kernel(
         nc.vector.quantize_mx(w_codes[:].bitcast(FP8X4), w_plane[:], w_bf[:].rearrange("p t m j -> p (t m j)"))
 
         x_codes = alloc("x_codes", [P, S], U32)
-        for u in range(2):
-            nc.vector.tensor_copy(x_codes[:, half_cols(u)], x_table[:].bitcast(U32).indirect(half_list(offs_l, u)))
+        for cols in HALVES:
+            nc.vector.tensor_copy(x_codes[:, cols], x_table[:].bitcast(U32).indirect(entries(offs_l, cols)))
 
-        def product_y(t, cols, y):
-            width = cols.stop - cols.start
-            bank = psum.tile([P, S], F32, name="bank")
-            rows = slice(t * P, (t + 1) * P)
-            nc.tensor.matmul_mx(
-                bank[:, :width], w_codes[:, rows].bitcast(FP8X4), w_plane[:, rows],
-                x_codes[:, cols].bitcast(FP8X4), x_plane[:, cols], start=True, stop=True,
-            )
-            nc.scalar.activation(y[:, cols], bank[:, :width], COPY)
-
-        def deal_bytes(a, tag):
-            dealt = alloc(f"dealt_bytes{a}", [P, H], U8, tag)
+        def deal_bytes(a, on):
+            dealt = alloc(f"dealt_bytes{a}", [P, H], U8, on)
             nc.vector.tensor_copy(
                 dealt[:].rearrange("p (t m) -> p m t", t=PACK),
                 d_picked_bytes[:, a * H : (a + 1) * H].rearrange("p (m t) -> p m t", t=PACK),
             )
-            for q in range(4):
+            for q in range(P // QUAD):
                 nc.sync.dma_start(
-                    d_plane[32 * q : 32 * q + 4, a * H : (a + 1) * H].bitcast(I32), dealt[32 * q : 32 * q + 32 : 8, :].bitcast(I32)
+                    d_plane[QUAD * q : QUAD * q + PACK, a * H : (a + 1) * H].bitcast(I32),
+                    dealt[QUAD * q : QUAD * (q + 1) : BLOCK, :].bitcast(I32),
                 )
 
         def deal_codes(dealt, picked, m0, t0, t1):
@@ -125,18 +130,21 @@ def tile_picked_daqhaarrelay_none_p_kernel(
         a_picked = [alloc(f"a_picked{u}", [P, HALF], U32) for u in range(2)]
         a_codes = alloc("a_codes", [P, H], U32)
         for u in range(2):
-            nc.vector.tensor_copy(a_picked[u][:], d_table[:].bitcast(U32).indirect(half_list(ka_l, u)))
+            nc.vector.tensor_copy(a_picked[u][:], d_table[:].bitcast(U32).indirect(entries(ka_l, HALVES[u])))
         for u in range(2):
-            deal_codes(a_codes, a_picked[u], u * 64, 0, PACK)
-
-        y_at = (3584, 2048, 5120, 2048)
-        sum_at = (None, 6144, 2560, None)
-        dt_on = ("a_picked0", "pb_neg0", "pa0", "pb_neg1")
+            deal_codes(a_codes, a_picked[u], u * P // 2, 0, PACK)
 
         def fetch_pairs(t):
-            y = relay.tile([P, S], F32, name=f"y{t}", offset=y_at[t], align_bytes=64)
-            for cols in (half_cols(0), half_cols(1)) if t == 0 else (slice(0, S),):
-                product_y(t, cols, y)
+            y = relay.tile([P, S], F32, name=f"y{t}", offset=Y_AT[t], align_bytes=64)
+            rows = slice(t * P, (t + 1) * P)
+            for cols in HALVES if t == 0 else (WHOLE,):
+                width = cols.stop - cols.start
+                bank = psum.tile([P, S], F32, name="bank")
+                nc.tensor.matmul_mx(
+                    bank[:, :width], w_codes[:, rows].bitcast(FP8X4), w_plane[:, rows],
+                    x_codes[:, cols].bitcast(FP8X4), x_plane[:, cols], start=True, stop=True,
+                )
+                nc.scalar.activation(y[:, cols], bank[:, :width], COPY)
             pa = alloc(f"pa{t}", [P, W], F32)
             pb_neg = alloc(f"pb_neg{t}", [P, W], F32)
             nc.scalar.activation(pa[:], y[:].indirect(n1_l[:]), COPY)
@@ -144,90 +152,109 @@ def tile_picked_daqhaarrelay_none_p_kernel(
             return pa, pb_neg
 
         def scale_pairs(t, pa, pb_neg):
-            if sum_at[t] is None:
-                pa_s = alloc(f"pa_s{t}", [P, W], F32)
+            if t in SCALED_AT:
+                pa_scaled = relay.tile([P, W], F32, name=f"pa_scaled{t}", offset=SCALED_AT[t], align_bytes=64)
             else:
-                pa_s = relay.tile([P, W], F32, name=f"pa_s{t}", offset=sum_at[t], align_bytes=64)
-            pb_s = alloc(f"pb_s{t}", [P, W], F32)
-            nc.scalar.activation(pa_s[:], pa[:], COPY, scale=0.75)
-            nc.scalar.activation(pb_s[:], pb_neg[:], COPY, scale=-0.75)
-            return pa_s, pb_s
+                pa_scaled = alloc(f"pa_scaled{t}", [P, W], F32)
+            pb_scaled = alloc(f"pb_scaled{t}", [P, W], F32)
+            nc.scalar.activation(pa_scaled[:], pa[:], COPY, scale=0.75)
+            nc.scalar.activation(pb_scaled[:], pb_neg[:], COPY, scale=-0.75)
+            return pa_scaled, pb_scaled
 
-        placed = []
+        dt_on = ("a_picked0", "pb_neg0", "pa0", "pb_neg1")
+        dts = []
 
-        def place_differences(t):
-            pa, pb_neg = fetch_pairs(t)
-            scaled = scale_pairs(t, pa, pb_neg) if t == 0 else None
+        def place_rb(t, pa, pb_neg):
             dt = alloc(f"dt{t}", [P, S], F32, dt_on[t])
             nc.vector.tensor_tensor(dt[:].indirect(n2_l[:]), pa[:], pb_neg[:], ADD)
-            placed.append((dt, pa, pb_neg, scaled))
+            dts.append(dt)
 
-        def place_sums(t):
-            dt, pa, pb_neg, scaled = placed[t]
-            pa_s, pb_s = scaled or scale_pairs(t, pa, pb_neg)
-            nc.vector.tensor_tensor(dt[:].indirect(n1_l[:]), pa_s[:], pb_s[:], ADD)
+        def place_ra(t, pa_scaled, pb_scaled):
+            nc.vector.tensor_tensor(dts[t][:].indirect(n1_l[:]), pa_scaled[:], pb_scaled[:], ADD)
 
-        place_differences(0)
+        fetched_pairs = [fetch_pairs(0)]
+        scaled = scale_pairs(0, *fetched_pairs[0])
+        place_rb(0, *fetched_pairs[0])
         deal_bytes(1, "a_picked1")
-        place_sums(0)
-        place_differences(1)
-        for t in range(1, PACK):
-            if t + 1 < PACK:
-                place_differences(t + 1)
-            place_sums(t)
+        place_ra(0, *scaled)
+        for t in range(1, PACK + 1):
+            if t < PACK:
+                fetched_pairs.append(fetch_pairs(t))
+                place_rb(t, *fetched_pairs[t])
+            if t > 1:
+                place_ra(t - 1, *scale_pairs(t - 1, *fetched_pairs[t - 1]))
 
-        pairs = [relay.tile([P, 2, 2 * HALF], BF16, name=f"pairs{u}", offset=(64, 4032)[u], align_bytes=64) for u in range(2)]
+        pairs = [
+            relay.tile([P, 2, 2 * HALF], BF16, name=f"pairs{u}", offset=PAIRS_AT[u], align_bytes=64) for u in range(2)
+        ]
         for t in range(PACK):
             for u in range(2):
-                nc.scalar.activation(pairs[u][:, t // 2, t % 2 :: 2], placed[t][0][:, half_cols(u)], COPY, scale=gain[:, t : t + 1])
+                nc.scalar.activation(pairs[u][:, t // 2, t % 2 :: 2], dts[t][:, HALVES[u]], COPY, scale=gain[:, t : t + 1])
 
-        b_picked = alloc("b_picked", [P, H], U32, f"pb_s{PACK - 2}")
+        b_picked = alloc("b_picked", [P, H], U32, f"pb_scaled{PACK - 2}")
         nc.vector.tensor_copy(b_picked[:], d_table[:].bitcast(U32).indirect(kb_l[:]))
         b_codes = alloc("b_codes", [P, H], U32, dt_on[PACK - 1])
 
         z_codes = alloc("z_codes", [P, S], U32)
         z_plane = alloc("z_plane", [P, S], U8)
-        for u in range(2):
+        for u, (t0, t1) in enumerate(((0, 1), (1, PACK))):
             z_bf = alloc(f"z_bf{u}", [P, HALF * PACK], BF16)
             nc.vector.tensor_copy(
                 z_bf[:].bitcast(I32).rearrange("p (c v) -> p c v", v=2),
                 pairs[u][:].bitcast(I32).rearrange("p v c -> p c v"),
             )
-            deal_codes(b_codes, b_picked, 0, *((0, 1), (1, PACK))[u])
-            nc.vector.quantize_mx(z_codes[:, half_cols(u)].bitcast(FP8X4), z_plane[:, half_cols(u)], z_bf[:])
+            deal_codes(b_codes, b_picked, 0, t0, t1)
+            nc.vector.quantize_mx(z_codes[:, HALVES[u]].bitcast(FP8X4), z_plane[:, HALVES[u]], z_bf[:])
 
-        out_rows = out.rearrange("(p t) c -> t p c", t=PACK)
-
-        def product_h(t, cols, h):
+        steps = ((0, HALVES[0]), (1, WHOLE), (0, HALVES[1]), (2, WHOLE), (3, WHOLE))
+        hs = [alloc(f"h{t}", [P, S], F32) for t in range(PACK)]
+        for t, cols in steps:
             width = cols.stop - cols.start
             bank = psum.tile([P, S], F32, name="bank")
-            rows = slice(t * P, (t + 1) * P)
             for a, codes in enumerate((a_codes, b_codes)):
                 nc.tensor.matmul_mx(
-                    bank[:, :width], codes[:, rows].bitcast(FP8X4), d_plane[:, a * H + t * P : a * H + (t + 1) * P],
+                    bank[:, :width], codes[:, t * P : (t + 1) * P].bitcast(FP8X4),
+                    d_plane[:, a * H + t * P : a * H + (t + 1) * P],
                     z_codes[:, cols].bitcast(FP8X4), z_plane[:, cols], start=(a == 0), stop=(a == 1),
                 )
-            nc.scalar.activation(h[:, cols], bank[:, :width], COPY, scale=0.0625)
+            nc.scalar.activation(hs[t][:, cols], bank[:, :width], COPY, scale=0.0625)
 
-        def finish(t, h, ds2, pieces):
-            for cols, lst in pieces:
-                width = cols.stop - cols.start
-                fetched = alloc(f"fetched{t}_{cols.start}", [P, width], F32)
-                nc.scalar.activation(fetched[:], ds2[:].indirect(lst), COPY)
-                res = alloc(f"res{t}_{cols.start}", [P, width], F32)
-                nc.vector.tensor_tensor(res[:], h[:, cols], fetched[:], MAX)
-                nc.sync.dma_start(out_rows[t][:, cols], res[:])
-
-        whole = lambda lst: [(slice(0, S), lst[:])]
-        halves = lambda lst: [(half_cols(u), half_list(lst, u)) for u in range(2)]
-        hs = [alloc(f"h{t}", [P, S], F32) for t in range(PACK)]
         ds2 = [alloc(f"ds2_{t}", [P, 2 * S], F32) for t in range(PACK)]
-        steps = [(0, *halves(n3_l)[0]), (1, *whole(n3_l)[0]), (0, *halves(n3_l)[1]), (2, *whole(n3_l)[0]), (3, *whole(n3_l)[0])]
-        for t, cols, lst in steps:
-            product_h(t, cols, hs[t])
-        after = {2: 1, 3: 0, 4: 2}
-        for n, (t, cols, lst) in enumerate(steps):
-            nc.vector.tensor_copy(ds2[t][:].indirect(lst), hs[t][:, cols])
-            if n in after:
-                finish(after[n], hs[after[n]], ds2[after[n]], whole(n4_l))
-        finish(3, hs[3], ds2[3], halves(n4_l))
+        out_rows = out.rearrange("(p t) c -> t p c", t=PACK)
+
+        def send(step):
+            t, cols = steps[step]
+            nc.vector.tensor_copy(ds2[t][:].indirect(entries(n3_l, cols)), hs[t][:, cols])
+
+        def fetch_excess(t):
+            fetched = alloc(f"fetched{t}", [P, S], F32)
+            nc.scalar.activation(fetched[:], ds2[t][:].indirect(n4_l[:]), COPY)
+            excess = alloc(f"excess{t}", [P, S], F32)
+            nc.gpsimd.tensor_tensor(excess[:], fetched[:], hs[t][:], SUBTRACT)
+            return excess
+
+        def store_raised(t, excess):
+            rise = alloc(f"rise{t}", [P, S], F32)
+            nc.scalar.activation(rise[:], excess[:], RELU)
+            result = alloc(f"result{t}", [P, S], F32)
+            nc.gpsimd.tensor_tensor(result[:], rise[:], hs[t][:], ADD)
+            nc.sync.dma_start(out_rows[t], result[:])
+
+        def store_largest(t, pieces, on):
+            fetched = alloc(f"fetched{t}", [P, S], F32, on)
+            result = alloc(f"result{t}", [P, S], F32)
+            for cols in pieces:
+                nc.scalar.activation(fetched[:, cols], ds2[t][:].indirect(entries(n4_l, cols)), COPY)
+                nc.vector.tensor_tensor(result[:, cols], hs[t][:, cols], fetched[:, cols], MAX)
+                nc.sync.dma_start(out_rows[t][:, cols], result[:, cols])
+
+        for step in range(3):
+            send(step)
+        excess1 = fetch_excess(1)
+        send(3)
+        excess0 = fetch_excess(0)
+        store_raised(1, excess1)
+        store_raised(0, excess0)
+        send(4)
+        store_largest(2, (WHOLE,), "excess1")
+        store_largest(3, HALVES, "excess0")

from contextlib import ExitStack

import concourse.mybir as mybir

K, T, S, H, W, G = 512, 2048, 512, 512, 256, 2048
FLOPS = 3 * 2 * K * H * S

F32 = mybir.dt.float32
BF16 = mybir.dt.bfloat16
I32 = mybir.dt.int32
U32 = mybir.dt.uint32
U16 = mybir.dt.uint16
U8 = mybir.dt.uint8
FP8X4 = mybir.dt.float8_e4m3fn_x4
COPY = mybir.ActivationFunctionType.Copy
RELU = mybir.ActivationFunctionType.Relu
ADD = mybir.AluOpType.add
SUBTRACT = mybir.AluOpType.subtract
MAX = mybir.AluOpType.max

P = 128
PACK = 4
QUAD = 32
BLOCK = 8
STRIPE = 16
HALF = S // 2
HALVES = (slice(0, HALF), slice(HALF, S))
WHOLE = slice(0, S)

ROW = 4 * S
EDGE = 64
Y_AT = (7 * ROW // 4, ROW, 5 * ROW // 2, ROW)
SCALED_AT = {1: 3 * ROW, 2: 5 * ROW // 4}
PAIRS_AT = (EDGE, 2 * ROW - EDGE)


def tile_picked_daqhaarrelay_none_p_kernel(
    tc, x_words, x_scales, w1, gs, d_words, d_scales, offs, n1, n2, ka, kb, n3, n4, out
):
    nc = tc.nc
    with ExitStack() as ctx:
        lists = ctx.enter_context(tc.tile_pool(name="lists", bufs=1))
        keep = ctx.enter_context(tc.tile_pool(name="keep", bufs=1))
        relay = ctx.enter_context(tc.tile_pool(name="relay", bufs=1))
        psum = ctx.enter_context(tc.psum_pool(name="psum", bufs=8))

        def alloc(name, shape, dtype, on=None):
            return keep.tile(shape, dtype, name=name, tag=on or name, align_bytes=64)

        def load_list(name, src):
            held = lists.tile(list(src.shape), U16, name=name)
            nc.sync.dma_start(held[:], src)
            return held

        def entries(held, cols):
            return held[:, cols.start // STRIPE : cols.stop // STRIPE]

        d_bytes = alloc("d_bytes", [P, G], U8)
        x_bytes = alloc("x_bytes", [P, T], U8)
        d_plane = alloc("d_plane", [P, 2 * H], U8)
        nc.vector.memset(x_bytes[:].bitcast(I32), 0)
        nc.gpsimd.memset(d_plane[:].bitcast(I32), 0)

        ka_l = load_list("ka_l", ka)
        nc.sync.dma_start(
            d_bytes[:].bitcast(I32), d_scales[0].bitcast(I32).unsqueeze(1).to_broadcast([P // BLOCK, BLOCK, G // 4])
        )
        kb_l = load_list("kb_l", kb)
        w_rows = w1.rearrange("(p j) c -> p j c", j=PACK)
        w_raw = [alloc(f"w_raw{u}", [P, PACK, HALF], F32) for u in range(2)]
        nc.sync.dma_start(w_raw[0][:], w_rows[:, :, HALVES[0]])
        for q in range(P // QUAD):
            nc.sync.dma_start(
                x_bytes[QUAD * q : QUAD * q + PACK, :].bitcast(I32), x_scales[0, PACK * q : PACK * (q + 1), :].bitcast(I32)
            )
        nc.sync.dma_start(w_raw[1][:], w_rows[:, :, HALVES[1]])
        offs_l = load_list("offs_l", offs)
        x_table = alloc("x_table", [P, T], I32)
        nc.sync.dma_start(x_table[:], x_words[0].rearrange("p n t -> p (n t)").bitcast(I32))
        n2_l = load_list("n2_l", n2)
        n1_l = load_list("n1_l", n1)
        d_table = alloc("d_table", [P, G], I32)
        nc.sync.dma_start(d_table[:], d_words[0].rearrange("p n t -> p (n t)").bitcast(I32))
        n3_l = load_list("n3_l", n3)
        n4_l = load_list("n4_l", n4)
        gain = alloc("gain", [P, PACK], F32)
        nc.sync.dma_start(gain[:], gs.rearrange("(p t) o -> p (t o)", t=PACK))

        d_picked_bytes = alloc("d_picked_bytes", [P, 2 * H], U8)
        for a, held in enumerate((ka_l, kb_l)):
            nc.vector.tensor_copy(d_picked_bytes[:, a * H : (a + 1) * H], d_bytes[:].indirect(held[:]))
        x_plane = alloc("x_plane", [P, S], U8)
        nc.vector.tensor_copy(x_plane[:], x_bytes[:].indirect(offs_l[:]))

        w_bf = alloc("w_bf", [P, PACK, P, PACK], BF16)
        for u in range(2):
            nc.scalar.activation(
                w_bf[:, :, u * P // 2 : (u + 1) * P // 2, :].rearrange("p t m j -> p m t j"),
                w_raw[u][:].rearrange("p j (m t) -> p m t j", t=PACK),
                COPY,
            )
        w_codes = alloc("w_codes", [P, H], U32)
        w_plane = alloc("w_plane", [P, H], U8)
        nc.vector.quantize_mx(w_codes[:].bitcast(FP8X4), w_plane[:], w_bf[:].rearrange("p t m j -> p (t m j)"))

        x_codes = alloc("x_codes", [P, S], U32)
        for cols in HALVES:
            nc.vector.tensor_copy(x_codes[:, cols], x_table[:].bitcast(U32).indirect(entries(offs_l, cols)))

        def deal_bytes(a, on):
            dealt = alloc(f"dealt_bytes{a}", [P, H], U8, on)
            nc.vector.tensor_copy(
                dealt[:].rearrange("p (t m) -> p m t", t=PACK),
                d_picked_bytes[:, a * H : (a + 1) * H].rearrange("p (m t) -> p m t", t=PACK),
            )
            for q in range(P // QUAD):
                nc.sync.dma_start(
                    d_plane[QUAD * q : QUAD * q + PACK, a * H : (a + 1) * H].bitcast(I32),
                    dealt[QUAD * q : QUAD * (q + 1) : BLOCK, :].bitcast(I32),
                )

        def deal_codes(dealt, picked, m0, t0, t1):
            count = picked.shape[1] // PACK
            nc.vector.tensor_copy(
                dealt[:].bitcast(I32).rearrange("p (t m) -> p m t", t=PACK)[:, m0 : m0 + count, t0:t1],
                picked[:].bitcast(I32).rearrange("p (m t) -> p m t", t=PACK)[:, :, t0:t1],
            )

        deal_bytes(0, "x_table")
        a_picked = [alloc(f"a_picked{u}", [P, HALF], U32) for u in range(2)]
        a_codes = alloc("a_codes", [P, H], U32)
        for u in range(2):
            nc.vector.tensor_copy(a_picked[u][:], d_table[:].bitcast(U32).indirect(entries(ka_l, HALVES[u])))
        for u in range(2):
            deal_codes(a_codes, a_picked[u], u * P // 2, 0, PACK)

        def fetch_pairs(t):
            y = relay.tile([P, S], F32, name=f"y{t}", offset=Y_AT[t], align_bytes=64)
            rows = slice(t * P, (t + 1) * P)
            for cols in HALVES if t == 0 else (WHOLE,):
                width = cols.stop - cols.start
                bank = psum.tile([P, S], F32, name="bank")
                nc.tensor.matmul_mx(
                    bank[:, :width], w_codes[:, rows].bitcast(FP8X4), w_plane[:, rows],
                    x_codes[:, cols].bitcast(FP8X4), x_plane[:, cols], start=True, stop=True,
                )
                nc.scalar.activation(y[:, cols], bank[:, :width], COPY)
            pa = alloc(f"pa{t}", [P, W], F32)
            pb_neg = alloc(f"pb_neg{t}", [P, W], F32)
            nc.scalar.activation(pa[:], y[:].indirect(n1_l[:]), COPY)
            nc.scalar.activation(pb_neg[:], y[:].indirect(n2_l[:]), COPY, scale=-1.0)
            return pa, pb_neg

        def scale_pairs(t, pa, pb_neg):
            if t in SCALED_AT:
                pa_scaled = relay.tile([P, W], F32, name=f"pa_scaled{t}", offset=SCALED_AT[t], align_bytes=64)
            else:
                pa_scaled = alloc(f"pa_scaled{t}", [P, W], F32)
            pb_scaled = alloc(f"pb_scaled{t}", [P, W], F32)
            nc.scalar.activation(pa_scaled[:], pa[:], COPY, scale=0.75)
            nc.scalar.activation(pb_scaled[:], pb_neg[:], COPY, scale=-0.75)
            return pa_scaled, pb_scaled

        dt_on = ("a_picked0", "pb_neg0", "pa0", "pb_neg1")
        dts = []

        def place_rb(t, pa, pb_neg):
            dt = alloc(f"dt{t}", [P, S], F32, dt_on[t])
            nc.vector.tensor_tensor(dt[:].indirect(n2_l[:]), pa[:], pb_neg[:], ADD)
            dts.append(dt)

        def place_ra(t, pa_scaled, pb_scaled):
            nc.vector.tensor_tensor(dts[t][:].indirect(n1_l[:]), pa_scaled[:], pb_scaled[:], ADD)

        fetched_pairs = [fetch_pairs(0)]
        scaled = scale_pairs(0, *fetched_pairs[0])
        place_rb(0, *fetched_pairs[0])
        deal_bytes(1, "a_picked1")
        place_ra(0, *scaled)
        for t in range(1, PACK + 1):
            if t < PACK:
                fetched_pairs.append(fetch_pairs(t))
                place_rb(t, *fetched_pairs[t])
            if t > 1:
                place_ra(t - 1, *scale_pairs(t - 1, *fetched_pairs[t - 1]))

        pairs = [
            relay.tile([P, 2, 2 * HALF], BF16, name=f"pairs{u}", offset=PAIRS_AT[u], align_bytes=64) for u in range(2)
        ]
        for t in range(PACK):
            for u in range(2):
                nc.scalar.activation(pairs[u][:, t // 2, t % 2 :: 2], dts[t][:, HALVES[u]], COPY, scale=gain[:, t : t + 1])

        b_picked = alloc("b_picked", [P, H], U32, f"pb_scaled{PACK - 2}")
        nc.vector.tensor_copy(b_picked[:], d_table[:].bitcast(U32).indirect(kb_l[:]))
        b_codes = alloc("b_codes", [P, H], U32, dt_on[PACK - 1])

        z_codes = alloc("z_codes", [P, S], U32)
        z_plane = alloc("z_plane", [P, S], U8)
        for u, (t0, t1) in enumerate(((0, 1), (1, PACK))):
            z_bf = alloc(f"z_bf{u}", [P, HALF * PACK], BF16)
            nc.vector.tensor_copy(
                z_bf[:].bitcast(I32).rearrange("p (c v) -> p c v", v=2),
                pairs[u][:].bitcast(I32).rearrange("p v c -> p c v"),
            )
            deal_codes(b_codes, b_picked, 0, t0, t1)
            nc.vector.quantize_mx(z_codes[:, HALVES[u]].bitcast(FP8X4), z_plane[:, HALVES[u]], z_bf[:])

        steps = ((0, HALVES[0]), (1, WHOLE), (0, HALVES[1]), (2, WHOLE), (3, WHOLE))
        hs = [alloc(f"h{t}", [P, S], F32) for t in range(PACK)]
        for t, cols in steps:
            width = cols.stop - cols.start
            bank = psum.tile([P, S], F32, name="bank")
            for a, codes in enumerate((a_codes, b_codes)):
                nc.tensor.matmul_mx(
                    bank[:, :width], codes[:, t * P : (t + 1) * P].bitcast(FP8X4),
                    d_plane[:, a * H + t * P : a * H + (t + 1) * P],
                    z_codes[:, cols].bitcast(FP8X4), z_plane[:, cols], start=(a == 0), stop=(a == 1),
                )
            nc.scalar.activation(hs[t][:, cols], bank[:, :width], COPY, scale=0.0625)

        ds2 = [alloc(f"ds2_{t}", [P, 2 * S], F32) for t in range(PACK)]
        out_rows = out.rearrange("(p t) c -> t p c", t=PACK)

        def send(step):
            t, cols = steps[step]
            nc.vector.tensor_copy(ds2[t][:].indirect(entries(n3_l, cols)), hs[t][:, cols])

        def fetch_excess(t):
            fetched = alloc(f"fetched{t}", [P, S], F32)
            nc.scalar.activation(fetched[:], ds2[t][:].indirect(n4_l[:]), COPY)
            excess = alloc(f"excess{t}", [P, S], F32)
            nc.gpsimd.tensor_tensor(excess[:], fetched[:], hs[t][:], SUBTRACT)
            return excess

        def store_raised(t, excess):
            rise = alloc(f"rise{t}", [P, S], F32)
            nc.scalar.activation(rise[:], excess[:], RELU)
            result = alloc(f"result{t}", [P, S], F32)
            nc.gpsimd.tensor_tensor(result[:], rise[:], hs[t][:], ADD)
            nc.sync.dma_start(out_rows[t], result[:])

        def store_largest(t, pieces, on):
            fetched = alloc(f"fetched{t}", [P, S], F32, on)
            result = alloc(f"result{t}", [P, S], F32)
            for cols in pieces:
                nc.scalar.activation(fetched[:, cols], ds2[t][:].indirect(entries(n4_l, cols)), COPY)
                nc.vector.tensor_tensor(result[:, cols], hs[t][:, cols], fetched[:, cols], MAX)
                nc.sync.dma_start(out_rows[t][:, cols], result[:, cols])

        for step in range(3):
            send(step)
        excess1 = fetch_excess(1)
        send(3)
        excess0 = fetch_excess(0)
        store_raised(1, excess1)
        store_raised(0, excess0)
        send(4)
        store_largest(2, (WHOLE,), "excess1")
        store_largest(3, HALVES, "excess0")
